import numpy as np
import ml_dtypes

BF16 = ml_dtypes.bfloat16


def bf(x):
    return np.asarray(x, np.float32).astype(BF16)


def f32(x):
    return np.asarray(x, np.float32)


def f64(x):
    return np.asarray(x).astype(np.float64)


def striped(idx):
    return np.tile(idx.reshape(-1, 16).T, (8, 1))


A, S, K, M, N, E, Q = 256, 256, 512, 384, 128, 1, 128


def setup_inputs():
    return {"a": bf(np.random.standard_normal((A, S))), "wd": bf(np.random.standard_normal((A, M)) / np.sqrt(A)), "x": bf(np.random.standard_normal((K, N))), "w": bf(1.2 * np.random.standard_normal((E, K, M)) / np.sqrt(K)), "s": f32(0.5 + np.random.random_sample((M, 1))), "offs": striped(np.random.permutation(S)[:N])}


def reference(a, wd, x, w, s, offs):
    idx = offs[:16].T.reshape(-1)
    z = f64(wd).T @ f64(a)
    for e in range(E):
        z[:, idx[e * Q : (e + 1) * Q]] += f64(w)[e].T @ f64(x)[:, e * Q : (e + 1) * Q]
    z = z / np.sqrt((z**2).mean(axis=0, keepdims=True) + 1e-5) * f64(s)
    return z

@@ -1,0 +1,73 @@
+import concourse.mybir as mybir
+
+P = 128
+D, K, M, N, COLS = 256, 512, 384, 128, 256
+EPS = 1e-5
+FLOPS = 2 * D * M * COLS + 2 * K * M * N + 5 * M * COLS
+
+BF16, F32, U16 = mybir.dt.bfloat16, mybir.dt.float32, mybir.dt.uint16
+MULT = mybir.AluOpType.mult
+SQUARE = mybir.ActivationFunctionType.Square
+ABS_RSQRT = mybir.ActivationFunctionType.Abs_reciprocal_sqrt
+
+
+def tile_rows_placenorm_proj_kernel(tc, a, wd, x, w, s, offs, out):
+    nc = tc.nc
+    d_blocks, k_blocks, m_blocks = D // P, K // P, M // P
+    half = k_blocks // 2
+    with (
+        tc.tile_pool(name="held", bufs=1) as held,
+        tc.psum_pool(name="psum", bufs=1) as psum,
+    ):
+        a_sb = held.tile([P, d_blocks, COLS], BF16, name="a_sb")
+        wd_sb = held.tile([P, d_blocks, M], BF16, name="wd_sb")
+        x_sb = held.tile([P, k_blocks, N], BF16, name="x_sb")
+        w_sb = [held.tile([P, half, M], BF16, name=f"w_sb{h}") for h in range(2)]
+        s_sb = held.tile([P, m_blocks], F32, name="s_sb")
+        offsets = held.tile([P, N // 16], U16, name="offsets")
+        ones = held.tile([P, P], BF16, name="ones")
+        eps = held.tile([P, 1], F32, name="eps")
+        early = held.tile([P, 1], F32, name="early")
+        rstd = held.tile([P, COLS], F32, name="rstd")
+        windows = [psum.tile([P, COLS], F32, name=f"window{m}") for m in range(m_blocks)]
+        sums = psum.tile([P, COLS], F32, name="sums")
+
+        w_rows = w.rearrange("e (p c) m -> p (e c) m", p=P)
+        nc.sync.dma_start(a_sb[:], a.rearrange("(p c) i -> p c i", p=P))
+        nc.sync.dma_start(wd_sb[:], wd.rearrange("(p c) m -> p c m", p=P))
+        nc.sync.dma_start(offsets[:], offs)
+        nc.sync.dma_start(x_sb[:], x.rearrange("(p c) j -> p c j", p=P))
+        nc.sync.dma_start(w_sb[0][:], w_rows[:, 0:half, :])
+        nc.sync.dma_start(w_sb[1][:], w_rows[:, half:k_blocks, :])
+        nc.scalar.dma_start(s_sb[:], s.rearrange("(a p) o -> p (a o)", p=P))
+
+        nc.vector.memset(eps[:], EPS)
+        nc.vector.memset(ones[:], 1.0)
+        nc.scalar.activation(early[:], eps[:], ABS_RSQRT, bias=eps[:])
+
+        for m in range(m_blocks):
+            for c in range(d_blocks):
+                nc.tensor.matmul(
+                    windows[m][:], wd_sb[:, c, m * P : (m + 1) * P], a_sb[:, c, :],
+                    start=(c == 0), stop=False,
+                )
+
+        for h in range(2):
+            for m in range(m_blocks):
+                for c in range(half):
+                    nc.tensor.matmul(
+                        windows[m][:].indirect(offsets[:]),
+                        w_sb[h][:, c, m * P : (m + 1) * P], x_sb[:, h * half + c, :],
+                        start=False, stop=(h == 1 and c == half - 1),
+                    )
+
+        for m in range(m_blocks):
+            squares = held.tile([P, COLS], BF16, name=f"squares{m}")
+            nc.scalar.activation(squares[:], windows[m][:], SQUARE)
+            nc.tensor.matmul(sums[:], ones[:], squares[:], start=(m == 0), stop=(m == m_blocks - 1))
+        nc.scalar.activation(rstd[:], sums[:], ABS_RSQRT, bias=eps[:], scale=1.0 / M)
+
+        for m in range(m_blocks):
+            normed = held.tile([P, COLS], F32, name=f"normed{m}")
+            nc.vector.scalar_tensor_tensor(normed[:], windows[m][:], s_sb[:, m : m + 1], rstd[:], MULT, MULT)
+            nc.sync.dma_start(out[m * P : (m + 1) * P, :], normed[:])

@@ -3,6 +3,8 @@ import concourse.mybir as mybir
 P = 128
 D, K, M, N, COLS = 256, 512, 384, 128, 256
 EPS = 1e-5
+BANK = 512
+WARM_UPS = 4
 FLOPS = 2 * D * M * COLS + 2 * K * M * N + 5 * M * COLS
 
 BF16, F32, U16 = mybir.dt.bfloat16, mybir.dt.float32, mybir.dt.uint16
@@ -31,6 +33,8 @@ def tile_rows_placenorm_proj_kernel(tc, a, wd, x, w, s, offs, out):
         rstd = held.tile([P, COLS], F32, name="rstd")
         windows = [psum.tile([P, COLS], F32, name=f"window{m}") for m in range(m_blocks)]
         sums = psum.tile([P, COLS], F32, name="sums")
+        spare = psum.tile([P, BANK], F32, name="spare")
+        zeros = held.tile([P, BANK], BF16, name="zeros")
 
         w_rows = w.rearrange("e (p c) m -> p (e c) m", p=P)
         nc.sync.dma_start(a_sb[:], a.rearrange("(p c) i -> p c i", p=P))
@@ -39,7 +43,11 @@ def tile_rows_placenorm_proj_kernel(tc, a, wd, x, w, s, offs, out):
         nc.sync.dma_start(x_sb[:], x.rearrange("(p c) j -> p c j", p=P))
         nc.sync.dma_start(w_sb[0][:], w_rows[:, 0:half, :])
         nc.sync.dma_start(w_sb[1][:], w_rows[:, half:k_blocks, :])
-        nc.scalar.dma_start(s_sb[:], s.rearrange("(a p) o -> p (a o)", p=P))
+        nc.sync.dma_start(s_sb[:], s.rearrange("(a p) o -> p (a o)", p=P))
+
+        nc.vector.memset(zeros[:], 0.0)
+        for i in range(WARM_UPS):
+            nc.tensor.matmul(spare[:], zeros[:, 0:P], zeros[:], start=True, stop=True)
 
         nc.vector.memset(eps[:], EPS)
         nc.vector.memset(ones[:], 1.0)

@@ -4,7 +4,7 @@ P = 128
 D, K, M, N, COLS = 256, 512, 384, 128, 256
 EPS = 1e-5
 BANK = 512
-WARM_UPS = 4
+WARM_UPS = 3
 FLOPS = 2 * D * M * COLS + 2 * K * M * N + 5 * M * COLS
 
 BF16, F32, U16 = mybir.dt.bfloat16, mybir.dt.float32, mybir.dt.uint16
@@ -17,12 +17,13 @@ def tile_rows_placenorm_proj_kernel(tc, a, wd, x, w, s, offs, out):
     nc = tc.nc
     d_blocks, k_blocks, m_blocks = D // P, K // P, M // P
     half = k_blocks // 2
+    halves = [slice(0, COLS // 2), slice(COLS // 2, COLS)]
     with (
         tc.tile_pool(name="held", bufs=1) as held,
         tc.psum_pool(name="psum", bufs=1) as psum,
     ):
-        a_sb = held.tile([P, d_blocks, COLS], BF16, name="a_sb")
-        wd_sb = held.tile([P, d_blocks, M], BF16, name="wd_sb")
+        a_sb = [held.tile([P, COLS], BF16, name=f"a_sb{c}") for c in range(d_blocks)]
+        wd_sb = [held.tile([P, M], BF16, name=f"wd_sb{c}") for c in range(d_blocks)]
         x_sb = held.tile([P, k_blocks, N], BF16, name="x_sb")
         w_sb = [held.tile([P, half, M], BF16, name=f"w_sb{h}") for h in range(2)]
         s_sb = held.tile([P, m_blocks], F32, name="s_sb")
@@ -30,15 +31,15 @@ def tile_rows_placenorm_proj_kernel(tc, a, wd, x, w, s, offs, out):
         ones = held.tile([P, P], BF16, name="ones")
         eps = held.tile([P, 1], F32, name="eps")
         early = held.tile([P, 1], F32, name="early")
-        rstd = held.tile([P, COLS], F32, name="rstd")
         windows = [psum.tile([P, COLS], F32, name=f"window{m}") for m in range(m_blocks)]
-        sums = psum.tile([P, COLS], F32, name="sums")
+        sums = [psum.tile([P, COLS // 2], F32, name=f"sums{h}") for h in range(2)]
         spare = psum.tile([P, BANK], F32, name="spare")
         zeros = held.tile([P, BANK], BF16, name="zeros")
 
         w_rows = w.rearrange("e (p c) m -> p (e c) m", p=P)
-        nc.sync.dma_start(a_sb[:], a.rearrange("(p c) i -> p c i", p=P))
-        nc.sync.dma_start(wd_sb[:], wd.rearrange("(p c) m -> p c m", p=P))
+        for c in range(d_blocks):
+            nc.sync.dma_start(a_sb[c][:], a[c * P : (c + 1) * P, :])
+            nc.sync.dma_start(wd_sb[c][:], wd[c * P : (c + 1) * P, :])
         nc.sync.dma_start(offsets[:], offs)
         nc.sync.dma_start(x_sb[:], x.rearrange("(p c) j -> p c j", p=P))
         nc.sync.dma_start(w_sb[0][:], w_rows[:, 0:half, :])
@@ -53,10 +54,10 @@ def tile_rows_placenorm_proj_kernel(tc, a, wd, x, w, s, offs, out):
         nc.vector.memset(ones[:], 1.0)
         nc.scalar.activation(early[:], eps[:], ABS_RSQRT, bias=eps[:])
 
-        for m in range(m_blocks):
-            for c in range(d_blocks):
+        for c in range(d_blocks):
+            for m in range(m_blocks):
                 nc.tensor.matmul(
-                    windows[m][:], wd_sb[:, c, m * P : (m + 1) * P], a_sb[:, c, :],
+                    windows[m][:], wd_sb[c][:, m * P : (m + 1) * P], a_sb[c][:],
                     start=(c == 0), stop=False,
                 )
 
@@ -69,13 +70,22 @@ def tile_rows_placenorm_proj_kernel(tc, a, wd, x, w, s, offs, out):
                         start=False, stop=(h == 1 and c == half - 1),
                     )
 
+        last = m_blocks - 1
         for m in range(m_blocks):
             squares = held.tile([P, COLS], BF16, name=f"squares{m}")
-            nc.scalar.activation(squares[:], windows[m][:], SQUARE)
-            nc.tensor.matmul(sums[:], ones[:], squares[:], start=(m == 0), stop=(m == m_blocks - 1))
-        nc.scalar.activation(rstd[:], sums[:], ABS_RSQRT, bias=eps[:], scale=1.0 / M)
+            for cols in halves if m == last else [slice(0, COLS)]:
+                nc.scalar.activation(squares[:, cols], windows[m][:, cols], SQUARE)
+            for h in range(2):
+                nc.tensor.matmul(sums[h][:], ones[:], squares[:, halves[h]], start=(m == 0), stop=(m == last))
 
+        normed = [held.tile([P, COLS], F32, name=f"normed{m}") for m in range(m_blocks)]
+        for h in range(2):
+            cols = halves[h]
+            rstd = held.tile([P, COLS // 2], F32, name=f"rstd{h}")
+            nc.scalar.activation(rstd[:], sums[h][:], ABS_RSQRT, bias=eps[:], scale=1.0 / M)
+            for m in range(m_blocks):
+                nc.vector.scalar_tensor_tensor(
+                    normed[m][:, cols], windows[m][:, cols], s_sb[:, m : m + 1], rstd[:], MULT, MULT
+                )
         for m in range(m_blocks):
-            normed = held.tile([P, COLS], F32, name=f"normed{m}")
-            nc.vector.scalar_tensor_tensor(normed[:], windows[m][:], s_sb[:, m : m + 1], rstd[:], MULT, MULT)
-            nc.sync.dma_start(out[m * P : (m + 1) * P, :], normed[:])
+            nc.sync.dma_start(out[m * P : (m + 1) * P, :], normed[m][:])

@@ -3,8 +3,7 @@ import concourse.mybir as mybir
 P = 128
 D, K, M, N, COLS = 256, 512, 384, 128, 256
 EPS = 1e-5
-BANK = 512
-WARM_UPS = 3
+WARM_UPS = 7
 FLOPS = 2 * D * M * COLS + 2 * K * M * N + 5 * M * COLS
 
 BF16, F32, U16 = mybir.dt.bfloat16, mybir.dt.float32, mybir.dt.uint16
@@ -33,8 +32,8 @@ def tile_rows_placenorm_proj_kernel(tc, a, wd, x, w, s, offs, out):
         early = held.tile([P, 1], F32, name="early")
         windows = [psum.tile([P, COLS], F32, name=f"window{m}") for m in range(m_blocks)]
         sums = [psum.tile([P, COLS // 2], F32, name=f"sums{h}") for h in range(2)]
-        spare = psum.tile([P, BANK], F32, name="spare")
-        zeros = held.tile([P, BANK], BF16, name="zeros")
+        spare = psum.tile([P, COLS], F32, name="spare")
+        zeros = held.tile([P, COLS], BF16, name="zeros")
 
         w_rows = w.rearrange("e (p c) m -> p (e c) m", p=P)
         for c in range(d_blocks):
@@ -61,14 +60,13 @@ def tile_rows_placenorm_proj_kernel(tc, a, wd, x, w, s, offs, out):
                     start=(c == 0), stop=False,
                 )
 
-        for h in range(2):
-            for m in range(m_blocks):
-                for c in range(half):
-                    nc.tensor.matmul(
-                        windows[m][:].indirect(offsets[:]),
-                        w_sb[h][:, c, m * P : (m + 1) * P], x_sb[:, h * half + c, :],
-                        start=False, stop=(h == 1 and c == half - 1),
-                    )
+        for m in range(m_blocks):
+            for k in range(k_blocks):
+                nc.tensor.matmul(
+                    windows[m][:].indirect(offsets[:]),
+                    w_sb[k // half][:, k % half, m * P : (m + 1) * P], x_sb[:, k, :],
+                    start=False, stop=(k == k_blocks - 1),
+                )
 
         last = m_blocks - 1
         for m in range(m_blocks):
@@ -78,14 +76,13 @@ def tile_rows_placenorm_proj_kernel(tc, a, wd, x, w, s, offs, out):
             for h in range(2):
                 nc.tensor.matmul(sums[h][:], ones[:], squares[:, halves[h]], start=(m == 0), stop=(m == last))
 
-        normed = [held.tile([P, COLS], F32, name=f"normed{m}") for m in range(m_blocks)]
         for h in range(2):
             cols = halves[h]
             rstd = held.tile([P, COLS // 2], F32, name=f"rstd{h}")
             nc.scalar.activation(rstd[:], sums[h][:], ABS_RSQRT, bias=eps[:], scale=1.0 / M)
             for m in range(m_blocks):
+                normed = held.tile([P, COLS // 2], F32, name=f"normed{m}_{h}")
                 nc.vector.scalar_tensor_tensor(
-                    normed[m][:, cols], windows[m][:, cols], s_sb[:, m : m + 1], rstd[:], MULT, MULT
+                    normed[:], windows[m][:, cols], s_sb[:, m : m + 1], rstd[:], MULT, MULT
                 )
-        for m in range(m_blocks):
-            nc.sync.dma_start(out[m * P : (m + 1) * P, :], normed[m][:])
+                nc.sync.dma_start(out[m * P : (m + 1) * P, cols], normed[:])

@@ -3,7 +3,7 @@ import concourse.mybir as mybir
 P = 128
 D, K, M, N, COLS = 256, 512, 384, 128, 256
 EPS = 1e-5
-WARM_UPS = 7
+WARM_UPS = 8
 FLOPS = 2 * D * M * COLS + 2 * K * M * N + 5 * M * COLS
 
 BF16, F32, U16 = mybir.dt.bfloat16, mybir.dt.float32, mybir.dt.uint16
@@ -21,8 +21,8 @@ def tile_rows_placenorm_proj_kernel(tc, a, wd, x, w, s, offs, out):
         tc.tile_pool(name="held", bufs=1) as held,
         tc.psum_pool(name="psum", bufs=1) as psum,
     ):
-        a_sb = [held.tile([P, COLS], BF16, name=f"a_sb{c}") for c in range(d_blocks)]
-        wd_sb = [held.tile([P, M], BF16, name=f"wd_sb{c}") for c in range(d_blocks)]
+        a_sb = held.tile([P, d_blocks, COLS], BF16, name="a_sb")
+        wd_sb = held.tile([P, d_blocks, M], BF16, name="wd_sb")
         x_sb = held.tile([P, k_blocks, N], BF16, name="x_sb")
         w_sb = [held.tile([P, half, M], BF16, name=f"w_sb{h}") for h in range(2)]
         s_sb = held.tile([P, m_blocks], F32, name="s_sb")
@@ -36,9 +36,8 @@ def tile_rows_placenorm_proj_kernel(tc, a, wd, x, w, s, offs, out):
         zeros = held.tile([P, COLS], BF16, name="zeros")
 
         w_rows = w.rearrange("e (p c) m -> p (e c) m", p=P)
-        for c in range(d_blocks):
-            nc.sync.dma_start(a_sb[c][:], a[c * P : (c + 1) * P, :])
-            nc.sync.dma_start(wd_sb[c][:], wd[c * P : (c + 1) * P, :])
+        nc.sync.dma_start(a_sb[:], a.rearrange("(p c) i -> p c i", p=P))
+        nc.sync.dma_start(wd_sb[:], wd.rearrange("(p c) m -> p c m", p=P))
         nc.sync.dma_start(offsets[:], offs)
         nc.sync.dma_start(x_sb[:], x.rearrange("(p c) j -> p c j", p=P))
         nc.sync.dma_start(w_sb[0][:], w_rows[:, 0:half, :])
@@ -53,10 +52,10 @@ def tile_rows_placenorm_proj_kernel(tc, a, wd, x, w, s, offs, out):
         nc.vector.memset(ones[:], 1.0)
         nc.scalar.activation(early[:], eps[:], ABS_RSQRT, bias=eps[:])
 
-        for c in range(d_blocks):
-            for m in range(m_blocks):
+        for m in range(m_blocks):
+            for c in range(d_blocks):
                 nc.tensor.matmul(
-                    windows[m][:], wd_sb[c][:, m * P : (m + 1) * P], a_sb[c][:],
+                    windows[m][:], wd_sb[:, c, m * P : (m + 1) * P], a_sb[:, c, :],
                     start=(c == 0), stop=False,
                 )
 

import concourse.mybir as mybir

P = 128
D, K, M, N, COLS = 256, 512, 384, 128, 256
EPS = 1e-5
WARM_UPS = 8
FLOPS = 2 * D * M * COLS + 2 * K * M * N + 5 * M * COLS

BF16, F32, U16 = mybir.dt.bfloat16, mybir.dt.float32, mybir.dt.uint16
MULT = mybir.AluOpType.mult
SQUARE = mybir.ActivationFunctionType.Square
ABS_RSQRT = mybir.ActivationFunctionType.Abs_reciprocal_sqrt


def tile_rows_placenorm_proj_kernel(tc, a, wd, x, w, s, offs, out):
    nc = tc.nc
    d_blocks, k_blocks, m_blocks = D // P, K // P, M // P
    half = k_blocks // 2
    halves = [slice(0, COLS // 2), slice(COLS // 2, COLS)]
    with (
        tc.tile_pool(name="held", bufs=1) as held,
        tc.psum_pool(name="psum", bufs=1) as psum,
    ):
        a_sb = held.tile([P, d_blocks, COLS], BF16, name="a_sb")
        wd_sb = held.tile([P, d_blocks, M], BF16, name="wd_sb")
        x_sb = held.tile([P, k_blocks, N], BF16, name="x_sb")
        w_sb = [held.tile([P, half, M], BF16, name=f"w_sb{h}") for h in range(2)]
        s_sb = held.tile([P, m_blocks], F32, name="s_sb")
        offsets = held.tile([P, N // 16], U16, name="offsets")
        ones = held.tile([P, P], BF16, name="ones")
        eps = held.tile([P, 1], F32, name="eps")
        early = held.tile([P, 1], F32, name="early")
        windows = [psum.tile([P, COLS], F32, name=f"window{m}") for m in range(m_blocks)]
        sums = [psum.tile([P, COLS // 2], F32, name=f"sums{h}") for h in range(2)]
        spare = psum.tile([P, COLS], F32, name="spare")
        zeros = held.tile([P, COLS], BF16, name="zeros")

        w_rows = w.rearrange("e (p c) m -> p (e c) m", p=P)
        nc.sync.dma_start(a_sb[:], a.rearrange("(p c) i -> p c i", p=P))
        nc.sync.dma_start(wd_sb[:], wd.rearrange("(p c) m -> p c m", p=P))
        nc.sync.dma_start(offsets[:], offs)
        nc.sync.dma_start(x_sb[:], x.rearrange("(p c) j -> p c j", p=P))
        nc.sync.dma_start(w_sb[0][:], w_rows[:, 0:half, :])
        nc.sync.dma_start(w_sb[1][:], w_rows[:, half:k_blocks, :])
        nc.sync.dma_start(s_sb[:], s.rearrange("(a p) o -> p (a o)", p=P))

        nc.vector.memset(zeros[:], 0.0)
        for i in range(WARM_UPS):
            nc.tensor.matmul(spare[:], zeros[:, 0:P], zeros[:], start=True, stop=True)

        nc.vector.memset(eps[:], EPS)
        nc.vector.memset(ones[:], 1.0)
        nc.scalar.activation(early[:], eps[:], ABS_RSQRT, bias=eps[:])

        for m in range(m_blocks):
            for c in range(d_blocks):
                nc.tensor.matmul(
                    windows[m][:], wd_sb[:, c, m * P : (m + 1) * P], a_sb[:, c, :],
                    start=(c == 0), stop=False,
                )

        for m in range(m_blocks):
            for k in range(k_blocks):
                nc.tensor.matmul(
                    windows[m][:].indirect(offsets[:]),
                    w_sb[k // half][:, k % half, m * P : (m + 1) * P], x_sb[:, k, :],
                    start=False, stop=(k == k_blocks - 1),
                )

        last = m_blocks - 1
        for m in range(m_blocks):
            squares = held.tile([P, COLS], BF16, name=f"squares{m}")
            for cols in halves if m == last else [slice(0, COLS)]:
                nc.scalar.activation(squares[:, cols], windows[m][:, cols], SQUARE)
            for h in range(2):
                nc.tensor.matmul(sums[h][:], ones[:], squares[:, halves[h]], start=(m == 0), stop=(m == last))

        for h in range(2):
            cols = halves[h]
            rstd = held.tile([P, COLS // 2], F32, name=f"rstd{h}")
            nc.scalar.activation(rstd[:], sums[h][:], ABS_RSQRT, bias=eps[:], scale=1.0 / M)
            for m in range(m_blocks):
                normed = held.tile([P, COLS // 2], F32, name=f"normed{m}_{h}")
                nc.vector.scalar_tensor_tensor(
                    normed[:], windows[m][:, cols], s_sb[:, m : m + 1], rstd[:], MULT, MULT
                )
                nc.sync.dma_start(out[m * P : (m + 1) * P, cols], normed[:])
